import numpy as np
import ml_dtypes


def mxq(x, axis, fmt="e4m3"):
    dtype, down = {"e4m3": (ml_dtypes.float8_e4m3fn, 7), "e5m2": (ml_dtypes.float8_e5m2, 14)}[fmt]
    v = np.moveaxis(np.asarray(x, np.float32).astype(ml_dtypes.bfloat16).astype(np.float64), axis, -1)
    blocks = v.reshape(v.shape[:-1] + (-1, 32))
    amax = np.abs(blocks).max(-1, keepdims=True)
    byte = np.maximum(np.where(amax > 0, np.frexp(amax)[1] - 1 + 127, 0) - down, 1)
    scale = np.exp2(byte - 127.0)
    codes = (blocks / scale).astype(np.float32).astype(dtype).astype(np.float64)
    return np.moveaxis((codes * scale).reshape(v.shape), -1, axis)


WIDE = False


def mx_kscale(k):
    if not WIDE:
        return np.ones(k)
    levels = np.array([10, -10, 5, -5, 0])
    if k % 512:
        return np.exp2(np.random.permutation(np.resize(levels, k // 32))).repeat(32)
    a = np.empty((k // 512, 16))
    for p in range(k // 512):
        a[p, :8] = np.random.permutation(np.resize(levels, 8))
        for g in range(8):
            far = levels[np.abs(levels - a[p, g]) >= 10]
            a[p, g + 8] = far[np.random.randint(len(far))]
    return np.exp2(a.ravel()).repeat(32)


def f64(x):
    return np.asarray(x).astype(np.float64)


def striped(idx):
    return np.tile(idx.reshape(-1, 16).T, (8, 1)).astype(np.uint16)


def unstriped(offs):
    return offs[:16].T.reshape(-1).astype(np.int64)


def striped8(idx):
    return np.concatenate([x.reshape(-1, 16).T for x in idx]).astype(np.uint16)


def runs(offs, k):
    lists = np.stack([offs[16 * r : 16 * r + 16].T.reshape(-1) for r in range(8)]).astype(np.int64)
    return lists[np.arange(k) % 512 // 64]


def pack_weight(w):
    k, n = w.shape
    w = f64(np.asarray(w, np.float32).astype(ml_dtypes.bfloat16)).reshape(k // 32, 32, n)
    amax = np.abs(w).max(1)
    byte = np.clip(np.where(amax > 0, np.frexp(amax)[1] - 1 + 127 - 7, 1), 1, 254)
    scaled = (w * np.exp2(127.0 - byte)[:, None, :]).reshape(k, n).astype(np.float32)
    words = np.ascontiguousarray(scaled.reshape(k // 512, 128, 4, n).transpose(0, 1, 3, 2)).astype(ml_dtypes.float8_e4m3fn).view(np.uint8)
    return words, np.ascontiguousarray(byte.astype(np.uint8).reshape(k // 512, 16, n))


def unpack_weight(words, scales):
    g, p, n, _ = words.shape
    vals = np.ascontiguousarray(words).view(ml_dtypes.float8_e4m3fn).astype(np.float64) * np.repeat(np.exp2(scales.astype(np.float64) - 127.0), 8, axis=1)[..., None]
    return vals.transpose(0, 1, 3, 2).reshape(g * 512, n)


def sigmoid(v):
    return 1.0 / (1.0 + np.exp(-np.maximum(v, -700.0)))

def planes(y):
    n, m = y.shape
    v = y.astype(np.float32).astype(ml_dtypes.bfloat16).astype(np.float64).reshape(n // 32, 32, m)
    top = np.abs(v).max(1)
    byte = np.clip(np.where(top > 0, np.frexp(top)[1] - 1 + 127 - 7, 1), 1, 254)
    codes = (v * np.exp2(127.0 - byte)[:, None, :]).reshape(n, m).astype(np.float32).astype(ml_dtypes.float8_e4m3fn).view(np.uint8)
    words = codes.reshape(n // 512, 128, 4, m).transpose(0, 1, 3, 2)
    return np.ascontiguousarray(words), np.ascontiguousarray(byte.astype(np.uint8).reshape(n // 512, 16, m))


K, T, S, V, N, C, H = 512, 2048, 512, 512, 512, 256, 512


def setup_inputs():
    n = np.random.standard_normal
    s = mx_kscale(K)[:, None]
    u = mx_kscale(S)
    packed_xT = pack_weight(n((K, T)) * s)
    packed_w1 = pack_weight(n((K, H)) / np.sqrt(K) / s)
    packed_w2 = pack_weight(n((K, H)) / np.sqrt(K) / s)
    return {
        "x_words": packed_xT[0],
        "x_scales": packed_xT[1],
        "w1_words": packed_w1[0],
        "w1_scales": packed_w1[1],
        "w2_words": packed_w2[0],
        "w2_scales": packed_w2[1],
        "gk": (np.random.uniform(0.5, 1.5, (H, 1)) * u[:, None]).astype(np.float32),
        "gq": (np.random.uniform(0.5, 1.5, (H, 1)) / u[:, None]).astype(np.float32),
        "fix": np.random.uniform(0.0, 1.5, (S, C)).astype(np.float32),
        "wv": (n((K, N)) / np.sqrt(K) / s).astype(np.float32),
        "gi": (np.random.uniform(0.5, 1.5, (S, 1)) / u[:, None]).astype(np.float32),
        "res": (1.5 * n((N, V))).astype(np.float32),
        "gt": (np.random.uniform(0.5, 1.5, (S, 1)) * u[:, None]).astype(np.float32),
        "offs": striped(np.random.permutation(T)[:S]),
        "qs": striped(np.random.permutation(T)[:V]),
        "at": striped8(np.stack([np.random.permutation(V)[:C] for _ in range(8)])),
    }


def reference(x_words, x_scales, w1_words, w1_scales, w2_words, w2_scales, gk, gq, fix, wv, gi, res, gt, offs, qs, at):
    xq = unpack_weight(x_words, x_scales)[:, unstriped(offs)]
    val = xq.T @ mxq(f64(wv), 0, "e4m3")
    zv = f64(gi) * val
    kf = unpack_weight(w1_words, w1_scales).T @ xq
    z = f64(gk) * kf
    x_qs = unpack_weight(x_words, x_scales)[:, unstriped(qs)]
    qf = unpack_weight(w2_words, w2_scales).T @ x_qs
    z2 = f64(gq) * qf
    s = 0.0625 * ((mxq(z, 0, "e4m3").T @ mxq(z2, 0, "e4m3")))
    p = sigmoid(s)
    nw = f64(fix) * (p[np.arange(S)[:, None], runs(at, S)])
    d = p.copy()
    d[np.arange(S)[:, None], runs(at, S)] = nw
    zp = f64(gt) * d
    out_0 = f64(res) + 0.0625 * ((mxq(zv, 0, "e4m3").T @ mxq(zp, 0, "e4m3")))
    return (out_0,) + planes(out_0)

@@ -1,0 +1,291 @@
+from contextlib import ExitStack
+
+import concourse.mybir as mybir
+
+F32 = mybir.dt.float32
+BF16 = mybir.dt.bfloat16
+I32 = mybir.dt.int32
+U32 = mybir.dt.uint32
+U16 = mybir.dt.uint16
+U8 = mybir.dt.uint8
+FP8X4 = mybir.dt.float8_e4m3fn_x4
+ACT = mybir.ActivationFunctionType
+ALU = mybir.AluOpType
+
+P = 128
+PACK = 4
+T = 2048
+D = 512
+C = 256
+CH = 128
+FLOPS = 5 * 2 * 512 * 512 * 512
+
+
+def tile_picked_attpatch_sigmoid_po_kernel(
+    tc, x_words, x_scales, w1_words, w1_scales, w2_words, w2_scales, gk, gq, fix, wv, gi, res, gt, offs, qs, at,
+    out_0, out_1, out_2,
+):
+    nc = tc.nc
+    with ExitStack() as ctx:
+        sb = ctx.enter_context(tc.tile_pool(name="sb", bufs=1))
+        ps = ctx.enter_context(tc.psum_pool(name="ps", bufs=1))
+
+        def tile(name, shape, dtype, tag=None):
+            return sb.tile(shape, dtype, name=name, tag=tag or name, align_bytes=64)
+
+        def bank(b):
+            return ps.tile([P, D], F32, name="bank%d" % b, tag="bank%d" % b)
+
+        def words_of(dram):
+            return dram[0].rearrange("p n t -> p (n t)").bitcast(I32)
+
+        def load_scale_rows(queue, dst, dram):
+            for q in range(4):
+                queue.dma_start(
+                    out=dst[32 * q : 32 * q + 32, :].bitcast(I32),
+                    in_=dram[0, 4 * q : 4 * q + 4, :].bitcast(I32).unsqueeze(0).broadcast_to([8, 4, dram.shape[2] // 4]),
+                )
+
+        def load_gain(queue, name, dram):
+            g = tile(name, [P, PACK], F32)
+            queue.dma_start(out=g[:], in_=dram.rearrange("(p t) o -> p (t o)", t=PACK))
+            return g
+
+        def mm(out, lw, ls, rw, rs):
+            nc.tensor.matmul_mx(out=out, lhsT=lw.bitcast(FP8X4), lhsT_scale=ls, rhs=rw.bitcast(FP8X4), rhs_scale=rs,
+                                start=True, stop=True)
+
+        def quant(words, scales, src):
+            nc.vector.quantize_mx(out=words.bitcast(FP8X4), scales=scales, in_=src)
+
+        offs_sb = tile("offs_sb", [P, D // 16], U16)
+        qs_sb = tile("qs_sb", [P, D // 16], U16)
+        at_sb = tile("at_sb", [P, C // 16], U16)
+
+        xs = tile("xs", [P, T], U8)
+        ws2_raw = tile("ws2_raw", [P, D], U8)
+        ws1_raw = tile("ws1_raw", [P, D], U8)
+        warm = tile("warm", [P, 2], F32)
+        nc.vector.memset(warm[:, 0:1], 0.0)
+        nc.scalar.activation(warm[:, 1:2], warm[:, 0:1], ACT.Sigmoid)
+
+        gq_sb = load_gain(nc.gpsimd, "gq_sb", gq)
+        gk_sb = load_gain(nc.gpsimd, "gk_sb", gk)
+        gi_sb = load_gain(nc.gpsimd, "gi_sb", gi)
+        gt_sb = load_gain(nc.gpsimd, "gt_sb", gt)
+        nc.sync.dma_start(qs_sb[:], qs)
+        load_scale_rows(nc.sync, xs[:], x_scales)
+        nc.sync.dma_start(offs_sb[:], offs)
+        xw = tile("xw", [P, T], U32)
+        nc.sync.dma_start(out=xw[:].bitcast(I32), in_=words_of(x_words))
+        w2_raw = tile("w2_raw", [P, D], U32)
+        nc.sync.dma_start(out=w2_raw[:].bitcast(I32), in_=words_of(w2_words))
+        load_scale_rows(nc.sync, ws2_raw[:], w2_scales)
+        load_scale_rows(nc.sync, ws1_raw[:], w1_scales)
+        w1_raw = tile("w1_raw", [P, D], U32)
+        nc.sync.dma_start(out=w1_raw[:].bitcast(I32), in_=words_of(w1_words))
+        wv_raw = tile("wv_raw", [P, PACK, D], F32)
+        nc.sync.dma_start(out=wv_raw[:], in_=wv.rearrange("(p j) m -> p j m", j=PACK))
+        nc.sync.dma_start(at_sb[:], at)
+        fix_sb = tile("fix_sb", [P, PACK, C], F32)
+        nc.sync.dma_start(out=fix_sb[:], in_=fix.rearrange("(p t) c -> p t c", t=PACK))
+        res_sb = tile("res_sb", [P, PACK, D], F32)
+        nc.sync.dma_start(out=res_sb[:], in_=res.rearrange("(p t) v -> p t v", t=PACK))
+
+        def deal(name, src, dtype, tag=None):
+            dst = tile(name, [P, D], dtype, tag)
+            nc.vector.tensor_copy(dst[:].rearrange("p (t m) -> p m t", t=PACK), src.rearrange("p (m t) -> p m t", t=PACK))
+            return dst
+
+        q_sc = tile("q_sc", [P, D], U8)
+        nc.vector.tensor_copy(q_sc[:], xs[:].indirect(qs_sb[:]))
+        k_sc_raw = tile("k_sc_raw", [P, D], U8)
+        nc.vector.tensor_copy(k_sc_raw[:], xs[:].indirect(offs_sb[:]))
+        w2_s = deal("w2_s", ws2_raw[:], U8)
+        k_sc = deal("k_sc", k_sc_raw[:], U8)
+        q_w = tile("q_w", [P, D], U32)
+        nc.vector.tensor_copy(q_w[:], xw[:].indirect(qs_sb[:]))
+        w2_w = deal("w2_w", w2_raw[:], U32, "ws2_raw")
+        k_w = tile("k_w", [P, D], U32, "w2_raw")
+        nc.vector.tensor_copy(k_w[:].rearrange("p (t m) -> p m t", t=PACK), xw[:].indirect(offs_sb[:]))
+        w1_s = deal("w1_s", ws1_raw[:], U8)
+        w1_w = deal("w1_w", w1_raw[:], U32)
+
+        def cols(j):
+            return slice(j * CH, (j + 1) * CH)
+
+        H = D // 2
+
+        def half(h):
+            return slice(h * H, (h + 1) * H)
+
+        def as_words(pair_tile):
+            return pair_tile[:].rearrange("p u c e -> p u (c e)").bitcast(F32)
+
+        z2_pl = [tile("z2_pl%d" % h, [P, PACK, H], BF16) for h in range(2)]
+        z2_bf = [tile("z2_bf%d" % h, [P, H, PACK], BF16) for h in range(2)]
+        z2_w = tile("z2_w", [P, D], U32)
+        z2_s = tile("z2_s", [P, D], U8)
+
+        def query_product(h):
+            for u in range(2):
+                b = bank(2 * h + u)
+                for e in range(2):
+                    t = 2 * u + e
+                    mm(b[:, half(e)], w2_w[:, cols(t)], w2_s[:, cols(t)], q_w[:, half(h)], q_sc[:, half(h)])
+                for e in range(2):
+                    t = 2 * u + e
+                    nc.scalar.activation(z2_pl[h][:, t, :], b[:, half(e)], ACT.Copy, scale=gq_sb[:, t : t + 1])
+
+        def query_weave(h):
+            nc.vector.tensor_copy(z2_bf[h][:], z2_pl[h][:].rearrange("p t c -> p c t"))
+
+        def query_quant(h):
+            quant(z2_w[:, half(h)], z2_s[:, half(h)], z2_bf[h][:].rearrange("p c t -> p (c t)"))
+
+        z_bf = [tile("z_bf%d" % j, [P, CH, PACK], BF16) for j in range(2)]
+        z_w = [tile("z_w%d" % j, [P, CH], U32) for j in range(2)]
+        z_s = [tile("z_s%d" % j, [P, CH], U8) for j in range(2)]
+        gk_b = gk_sb[:].unsqueeze(1).to_broadcast([P, CH, PACK])
+
+        def key_product(j):
+            b = bank(4 + j)
+            for t in range(PACK):
+                mm(b[:, cols(t)], w1_w[:, cols(t)], w1_s[:, cols(t)], k_w[:, cols(j)], k_sc[:, cols(j)])
+            nc.vector.tensor_tensor(z_bf[j][:], b[:].rearrange("p (t c) -> p c t", t=PACK), gk_b, ALU.mult)
+
+        def key_quant(j):
+            quant(z_w[j][:], z_s[j][:], z_bf[j][:].rearrange("p c t -> p (c t)"))
+
+        zl_pair = tile("zl_pair", [P, 2, H, 2], BF16)
+        zl_bf = tile("zl_bf", [P, H, 2], F32)
+        zl_w = tile("zl_w", [P, H], U32)
+        zl_s = tile("zl_s", [P, H], U8)
+
+        def late_keys():
+            for u in range(2):
+                b = bank(6 + u)
+                for e in range(2):
+                    t = 2 * u + e
+                    mm(b[:, half(e)], w1_w[:, cols(t)], w1_s[:, cols(t)], k_w[:, half(1)], k_sc[:, half(1)])
+                for e in range(2):
+                    t = 2 * u + e
+                    nc.scalar.activation(zl_pair[:, u, :, e], b[:, half(e)], ACT.Copy, scale=gk_sb[:, t : t + 1])
+
+        query_product(0)
+        query_product(1)
+        query_weave(0)
+        key_product(0)
+        query_quant(0)
+        query_weave(1)
+        key_quant(0)
+        query_quant(1)
+        key_product(1)
+        late_keys()
+        key_quant(1)
+        key_w = [z_w[0][:], z_w[1][:], zl_w[:, cols(0)], zl_w[:, cols(1)]]
+        key_s = [z_s[0][:], z_s[1][:], zl_s[:, cols(0)], zl_s[:, cols(1)]]
+
+        wv_bf = tile("wv_bf", [P, D, PACK], BF16)
+        wv_w = tile("wv_w", [P, D], U32)
+        wv_s = tile("wv_s", [P, D], U8)
+
+        p_sb = [tile("p%d" % j, [P, D], F32) for j in range(PACK)]
+        pg = [tile("pg%d" % j, [P, C], F32) for j in range(PACK)]
+        zp_pair = tile("zp_pair", [P, 2, D, 2], BF16)
+        zv_pair = tile("zv_pair", [P, 2, D, 2], BF16)
+
+        def score(j):
+            b = bank(j)
+            mm(b[:], key_w[j], key_s[j], z2_w[:], z2_s[:])
+            nc.scalar.activation(p_sb[j][:], b[:], ACT.Sigmoid, scale=0.0625)
+
+        def fetch(j):
+            nc.vector.tensor_copy(pg[j][:], p_sb[j][:].indirect(at_sb[:]))
+
+        def put(j):
+            nc.vector.tensor_tensor(p_sb[j][:].indirect(at_sb[:]), pg[j][:], fix_sb[:, j, :], ALU.mult)
+
+        def weigh(j):
+            nc.scalar.activation(zp_pair[:, j // 2, :, j % 2], p_sb[j][:], ACT.Copy, scale=gt_sb[:, j : j + 1])
+
+        def value(t):
+            b = bank(4 + t)
+            mm(b[:], k_w[:, cols(t)], k_sc[:, cols(t)], wv_w[:], wv_s[:])
+            nc.scalar.activation(
+                zv_pair[:, t // 2, :, t % 2].rearrange("p (u m) -> p u m", u=PACK),
+                b[:].rearrange("p (m u) -> p u m", u=PACK), ACT.Copy, scale=gi_sb[:, t : t + 1])
+
+        def wv_weave(h):
+            nc.scalar.copy(wv_bf[:, half(h), :], wv_raw[:, :, half(h)].rearrange("p j m -> p m j"))
+
+        score(0)
+        score(1)
+        nc.vector.tensor_copy(zl_bf[:], as_words(zl_pair).rearrange("p u c -> p c u"))
+        fetch(0)
+        quant(zl_w[:], zl_s[:], zl_bf[:].rearrange("p c u -> p (c u)").bitcast(BF16))
+        wv_weave(0)
+        wv_weave(1)
+        put(0)
+        fetch(1)
+        score(2)
+        score(3)
+        quant(wv_w[:], wv_s[:], wv_bf[:].rearrange("p c t -> p (c t)"))
+        put(1)
+        fetch(2)
+        fetch(3)
+        for t in range(PACK):
+            value(t)
+        put(2)
+        weigh(0)
+        weigh(1)
+        zv_bf = tile("zv_bf", [P, D, 2], F32)
+        nc.vector.tensor_copy(
+            zv_bf[:], zv_pair[:].rearrange("p u c e -> p u (c e)").bitcast(F32).rearrange("p u c -> p c u"))
+        weigh(2)
+        put(3)
+        zv_w = tile("zv_w", [P, D], U32)
+        zv_s = tile("zv_s", [P, D], U8)
+        quant(zv_w[:], zv_s[:], zv_bf[:].rearrange("p c u -> p (c u)").bitcast(BF16))
+        weigh(3)
+
+        zp_words = zp_pair[:].rearrange("p u c e -> p u (c e)").bitcast(F32)
+        zp_bf = [tile("zp_bf%d" % h, [P, H, 2], F32) for h in range(2)]
+        zp_w = [tile("zp_w%d" % h, [P, H], U32) for h in range(2)]
+        zp_s = [tile("zp_s%d" % h, [P, H], U8) for h in range(2)]
+        for h in range(2):
+            nc.vector.tensor_copy(zp_bf[h][:], zp_words[:, :, h * H : (h + 1) * H].rearrange("p u c -> p c u"))
+        for h in range(2):
+            quant(zp_w[h][:], zp_s[h][:], zp_bf[h][:].rearrange("p c u -> p (c u)").bitcast(BF16))
+
+        y_w = tile("y_w", [P, D], U32)
+        y_s = tile("y_s", [P, D], U8)
+        out_v = out_0.rearrange("(p t) v -> p t v", t=PACK)
+        y_bf = [tile("y_bf%d" % j, [P, CH, PACK], BF16) for j in range(PACK)]
+
+        def out_chunk(j):
+            b = bank(j)
+            h, o = divmod(j, 2)
+            for t in range(PACK):
+                mm(b[:, cols(t)], zv_w[:, cols(t)], zv_s[:, cols(t)], zp_w[h][:, cols(o)], zp_s[h][:, cols(o)])
+            y = tile("y%d" % j, [P, PACK, CH], F32)
+            nc.vector.scalar_tensor_tensor(
+                y[:], b[:].rearrange("p (t c) -> p t c", t=PACK), 0.0625, res_sb[:, :, cols(j)], ALU.mult, ALU.add)
+            nc.sync.dma_start(out=out_v[:, :, cols(j)], in_=y[:])
+            nc.scalar.copy(y_bf[j][:], y[:].rearrange("p t c -> p c t"))
+
+        def out_quant(j):
+            quant(y_w[:, cols(j)], y_s[:, cols(j)], y_bf[j][:].rearrange("p c t -> p (c t)"))
+
+        out_chunk(0)
+        out_chunk(1)
+        out_chunk(2)
+        out_quant(0)
+        out_chunk(3)
+        out_quant(1)
+        out_quant(2)
+        out_quant(3)
+        nc.sync.dma_start(out=words_of(out_1), in_=y_w[:].bitcast(I32))
+        for q in range(4):
+            queue = nc.scalar if q % 2 else nc.sync
+            queue.dma_start(out=out_2[0, 4 * q : 4 * q + 4, :].bitcast(I32), in_=y_s[32 * q : 32 * q + 4, :].bitcast(I32))

@@ -13,12 +13,17 @@ ACT = mybir.ActivationFunctionType
 ALU = mybir.AluOpType
 
 P = 128
-PACK = 4
-T = 2048
+SLOTS = 4
+BLOCK_PARTS = 8
+QUADRANTS = 4
+LIST_ROWS = 16
+TOKENS = 2048
 D = 512
-C = 256
-CH = 128
-FLOPS = 5 * 2 * 512 * 512 * 512
+HALF = D // 2
+CHUNK = 128
+PATCH = 256
+SIXTEENTH = 0.0625
+FLOPS = 5 * 2 * D * D * D
 
 
 def tile_picked_attpatch_sigmoid_po_kernel(
@@ -30,262 +35,299 @@ def tile_picked_attpatch_sigmoid_po_kernel(
         sb = ctx.enter_context(tc.tile_pool(name="sb", bufs=1))
         ps = ctx.enter_context(tc.psum_pool(name="ps", bufs=1))
 
-        def tile(name, shape, dtype, tag=None):
-            return sb.tile(shape, dtype, name=name, tag=tag or name, align_bytes=64)
+        def tile(name, shape, dtype, after=None):
+            return sb.tile(shape, dtype, name=name, tag=after or name, align_bytes=64)
 
-        def bank(b):
-            return ps.tile([P, D], F32, name="bank%d" % b, tag="bank%d" % b)
+        def bank(number):
+            return ps.tile([P, D], F32, name="bank%d" % number, tag="bank%d" % number)
+
+        def chunk(j):
+            return slice(j * CHUNK, (j + 1) * CHUNK)
+
+        def half(s):
+            return slice(s * HALF, (s + 1) * HALF)
 
         def words_of(dram):
             return dram[0].rearrange("p n t -> p (n t)").bitcast(I32)
 
+        def product(out, lhs_words, lhs_scales, rhs_words, rhs_scales):
+            nc.tensor.matmul_mx(out=out, lhsT=lhs_words.bitcast(FP8X4), lhsT_scale=lhs_scales,
+                                rhs=rhs_words.bitcast(FP8X4), rhs_scale=rhs_scales, start=True, stop=True)
+
+        def quantise(words, scales, woven):
+            nc.vector.quantize_mx(out=words.bitcast(FP8X4), scales=scales, in_=woven.rearrange("p c t -> p (c t)"))
+
+        def weave_planes(copy, woven, planes):
+            copy(woven.rearrange("p (c n) t -> p c t n", n=4), planes.rearrange("p t (c n) -> p c t n", n=4))
+
+        def weave_pairs(copy, woven, pairs):
+            copy(woven.rearrange("p c t -> p (c t)").bitcast(F32).rearrange("p (c u) -> p c u", u=2),
+                 pairs.rearrange("p u c e -> p u (c e)").bitcast(F32).rearrange("p u c -> p c u"))
+
         def load_scale_rows(queue, dst, dram):
-            for q in range(4):
-                queue.dma_start(
-                    out=dst[32 * q : 32 * q + 32, :].bitcast(I32),
-                    in_=dram[0, 4 * q : 4 * q + 4, :].bitcast(I32).unsqueeze(0).broadcast_to([8, 4, dram.shape[2] // 4]),
-                )
+            repeats = P // QUADRANTS // 4
+            for q in range(QUADRANTS):
+                rows = dram[0, 4 * q : 4 * q + 4, :].bitcast(I32)
+                queue.dma_start(out=dst[32 * q : 32 * q + 32, :].bitcast(I32),
+                                in_=rows.unsqueeze(0).broadcast_to([repeats, 4, dram.shape[2] // 4]))
 
-        def load_gain(queue, name, dram):
-            g = tile(name, [P, PACK], F32)
-            queue.dma_start(out=g[:], in_=dram.rearrange("(p t) o -> p (t o)", t=PACK))
-            return g
+        def load_feature_gain(name, dram):
+            gain = tile(name, [P, SLOTS], F32)
+            nc.gpsimd.dma_start(out=gain[:], in_=dram.rearrange("(p t) o -> p (t o)", t=SLOTS))
+            return gain
 
-        def mm(out, lw, ls, rw, rs):
-            nc.tensor.matmul_mx(out=out, lhsT=lw.bitcast(FP8X4), lhsT_scale=ls, rhs=rw.bitcast(FP8X4), rhs_scale=rs,
-                                start=True, stop=True)
+        def load_entry_gain(name, dram):
+            gain = tile(name, [P, SLOTS, 8], F32)
+            rows = dram.rearrange("(b t r) o -> t b r o", t=SLOTS, r=BLOCK_PARTS)
+            with nc.allow_non_contiguous_dma(reason="one value a partition"):
+                for t in range(SLOTS):
+                    nc.sync.dma_start(out=gain[:, t, 0:1], in_=rows[t])
+            return gain
 
-        def quant(words, scales, src):
-            nc.vector.quantize_mx(out=words.bitcast(FP8X4), scales=scales, in_=src)
+        offs_sb = tile("offs_sb", [P, D // LIST_ROWS], U16)
+        qs_sb = tile("qs_sb", [P, D // LIST_ROWS], U16)
+        at_sb = tile("at_sb", [P, PATCH // LIST_ROWS], U16)
+        x_scale_table = tile("x_scale_table", [P, TOKENS], U8)
+        w2_scales_in = tile("w2_scales_in", [P, D], U8)
+        w1_scales_in = tile("w1_scales_in", [P, D], U8)
 
-        offs_sb = tile("offs_sb", [P, D // 16], U16)
-        qs_sb = tile("qs_sb", [P, D // 16], U16)
-        at_sb = tile("at_sb", [P, C // 16], U16)
-
-        xs = tile("xs", [P, T], U8)
-        ws2_raw = tile("ws2_raw", [P, D], U8)
-        ws1_raw = tile("ws1_raw", [P, D], U8)
         warm = tile("warm", [P, 2], F32)
         nc.vector.memset(warm[:, 0:1], 0.0)
         nc.scalar.activation(warm[:, 1:2], warm[:, 0:1], ACT.Sigmoid)
 
-        gq_sb = load_gain(nc.gpsimd, "gq_sb", gq)
-        gk_sb = load_gain(nc.gpsimd, "gk_sb", gk)
-        gi_sb = load_gain(nc.gpsimd, "gi_sb", gi)
-        gt_sb = load_gain(nc.gpsimd, "gt_sb", gt)
+        gq_sb = load_feature_gain("gq_sb", gq)
+        gk_sb = load_feature_gain("gk_sb", gk)
         nc.sync.dma_start(qs_sb[:], qs)
-        load_scale_rows(nc.sync, xs[:], x_scales)
+        load_scale_rows(nc.sync, x_scale_table[:], x_scales)
         nc.sync.dma_start(offs_sb[:], offs)
-        xw = tile("xw", [P, T], U32)
-        nc.sync.dma_start(out=xw[:].bitcast(I32), in_=words_of(x_words))
-        w2_raw = tile("w2_raw", [P, D], U32)
-        nc.sync.dma_start(out=w2_raw[:].bitcast(I32), in_=words_of(w2_words))
-        load_scale_rows(nc.sync, ws2_raw[:], w2_scales)
-        load_scale_rows(nc.sync, ws1_raw[:], w1_scales)
-        w1_raw = tile("w1_raw", [P, D], U32)
-        nc.sync.dma_start(out=w1_raw[:].bitcast(I32), in_=words_of(w1_words))
-        wv_raw = tile("wv_raw", [P, PACK, D], F32)
-        nc.sync.dma_start(out=wv_raw[:], in_=wv.rearrange("(p j) m -> p j m", j=PACK))
+        w2_words_in = tile("w2_words_in", [P, D], U32)
+        nc.sync.dma_start(out=w2_words_in[:].bitcast(I32), in_=words_of(w2_words))
+        x_word_table = tile("x_word_table", [P, TOKENS], U32)
+        nc.sync.dma_start(out=x_word_table[:].bitcast(I32), in_=words_of(x_words))
+        load_scale_rows(nc.scalar, w2_scales_in[:], w2_scales)
+        w1_words_in = tile("w1_words_in", [P, D], U32)
+        nc.sync.dma_start(out=w1_words_in[:].bitcast(I32), in_=words_of(w1_words))
+        load_scale_rows(nc.sync, w1_scales_in[:], w1_scales)
+        wv_in = tile("wv_in", [P, SLOTS, D], F32)
+        nc.sync.dma_start(out=wv_in[:], in_=wv.rearrange("(p t) m -> p t m", t=SLOTS))
         nc.sync.dma_start(at_sb[:], at)
-        fix_sb = tile("fix_sb", [P, PACK, C], F32)
-        nc.sync.dma_start(out=fix_sb[:], in_=fix.rearrange("(p t) c -> p t c", t=PACK))
-        res_sb = tile("res_sb", [P, PACK, D], F32)
-        nc.sync.dma_start(out=res_sb[:], in_=res.rearrange("(p t) v -> p t v", t=PACK))
+        fix_sb = [tile("fix%d" % t, [P, PATCH], F32) for t in range(SLOTS)]
+        fix_rows = fix.rearrange("(b t r) c -> t b r c", t=SLOTS, r=BLOCK_PARTS)
+        for t in range(SLOTS):
+            nc.sync.dma_start(out=fix_sb[t][:], in_=fix_rows[t])
+        res_sb = tile("res_sb", [P, SLOTS, D], F32)
+        nc.sync.dma_start(out=res_sb[:], in_=res.rearrange("(p t) v -> p t v", t=SLOTS))
+        gi_sb = load_entry_gain("gi_sb", gi)
+        gt_sb = load_entry_gain("gt_sb", gt)
 
-        def deal(name, src, dtype, tag=None):
-            dst = tile(name, [P, D], dtype, tag)
-            nc.vector.tensor_copy(dst[:].rearrange("p (t m) -> p m t", t=PACK), src.rearrange("p (m t) -> p m t", t=PACK))
-            return dst
+        def deal_weight_words(name, src, after=None):
+            dealt = tile(name, [P, D], U32, after)
+            nc.vector.tensor_copy(dealt[:].rearrange("p (t a n) -> p a t n", t=SLOTS, n=4),
+                                  src.rearrange("p (a n t) -> p a t n", t=SLOTS, n=4))
+            return dealt
 
-        q_sc = tile("q_sc", [P, D], U8)
-        nc.vector.tensor_copy(q_sc[:], xs[:].indirect(qs_sb[:]))
-        k_sc_raw = tile("k_sc_raw", [P, D], U8)
-        nc.vector.tensor_copy(k_sc_raw[:], xs[:].indirect(offs_sb[:]))
-        w2_s = deal("w2_s", ws2_raw[:], U8)
-        k_sc = deal("k_sc", k_sc_raw[:], U8)
-        q_w = tile("q_w", [P, D], U32)
-        nc.vector.tensor_copy(q_w[:], xw[:].indirect(qs_sb[:]))
-        w2_w = deal("w2_w", w2_raw[:], U32, "ws2_raw")
-        k_w = tile("k_w", [P, D], U32, "w2_raw")
-        nc.vector.tensor_copy(k_w[:].rearrange("p (t m) -> p m t", t=PACK), xw[:].indirect(offs_sb[:]))
-        w1_s = deal("w1_s", ws1_raw[:], U8)
-        w1_w = deal("w1_w", w1_raw[:], U32)
+        def deal_weight_scales(name, src):
+            dealt = tile(name, [P, D], U8)
+            nc.vector.tensor_copy(dealt[:].rearrange("p (t c) -> p t c", t=SLOTS),
+                                  src.rearrange("p (c t) -> p t c", t=SLOTS))
+            return dealt
 
-        def cols(j):
-            return slice(j * CH, (j + 1) * CH)
+        xq_scales = tile("xq_scales", [P, D], U8)
+        nc.vector.tensor_copy(xq_scales[:], x_scale_table[:].indirect(qs_sb[:]))
+        xk_scales_listed = tile("xk_scales_listed", [P, D], U8)
+        nc.vector.tensor_copy(xk_scales_listed[:], x_scale_table[:].indirect(offs_sb[:]))
+        w2_s = deal_weight_scales("w2_s", w2_scales_in[:])
+        xk_scales = tile("xk_scales", [P, D], U8)
+        nc.vector.tensor_copy(xk_scales[:].bitcast(I32).rearrange("p (t b w) -> p t b w", t=SLOTS, w=2),
+                              xk_scales_listed[:].bitcast(I32).rearrange("p (b t w) -> p t b w", t=SLOTS, w=2))
+        w2_w = deal_weight_words("w2_w", w2_words_in[:], after="w2_scales_in")
+        xq_words = tile("xq_words", [P, D], U32, after="w2_words_in")
+        list_half = HALF // LIST_ROWS
+        for s in range(2):
+            nc.vector.tensor_copy(xq_words[:, half(s)],
+                                  x_word_table[:].indirect(qs_sb[:, s * list_half : (s + 1) * list_half]))
+        xk_words = tile("xk_words", [P, D], U32)
+        nc.vector.tensor_copy(xk_words[:].rearrange("p (t b r) -> p b t r", t=SLOTS, r=BLOCK_PARTS),
+                              x_word_table[:].indirect(offs_sb[:]))
+        w1_w = deal_weight_words("w1_w", w1_words_in[:])
+        w1_s = deal_weight_scales("w1_s", w1_scales_in[:])
 
-        H = D // 2
-
-        def half(h):
-            return slice(h * H, (h + 1) * H)
-
-        def as_words(pair_tile):
-            return pair_tile[:].rearrange("p u c e -> p u (c e)").bitcast(F32)
-
-        z2_pl = [tile("z2_pl%d" % h, [P, PACK, H], BF16) for h in range(2)]
-        z2_bf = [tile("z2_bf%d" % h, [P, H, PACK], BF16) for h in range(2)]
-        z2_w = tile("z2_w", [P, D], U32)
-        z2_s = tile("z2_s", [P, D], U8)
-
-        def query_product(h):
+        def scaled_half(first_bank, weight_words, weight_scales, x_words_half, x_scales_half, gain, destination):
             for u in range(2):
-                b = bank(2 * h + u)
+                acc = bank(first_bank + u)
                 for e in range(2):
                     t = 2 * u + e
-                    mm(b[:, half(e)], w2_w[:, cols(t)], w2_s[:, cols(t)], q_w[:, half(h)], q_sc[:, half(h)])
+                    product(acc[:, half(e)], weight_words[:, chunk(t)], weight_scales[:, chunk(t)],
+                            x_words_half, x_scales_half)
                 for e in range(2):
                     t = 2 * u + e
-                    nc.scalar.activation(z2_pl[h][:, t, :], b[:, half(e)], ACT.Copy, scale=gq_sb[:, t : t + 1])
+                    nc.scalar.activation(destination(t), acc[:, half(e)], ACT.Copy, scale=gain[:, t : t + 1])
 
-        def query_weave(h):
-            nc.vector.tensor_copy(z2_bf[h][:], z2_pl[h][:].rearrange("p t c -> p c t"))
+        z2_planes = [tile("z2_planes%d" % s, [P, SLOTS, HALF], BF16) for s in range(2)]
+        z2_woven = [tile("z2_woven0", [P, HALF, SLOTS], BF16, after="w1_scales_in"),
+                    tile("z2_woven1", [P, HALF, SLOTS], BF16)]
+        z2_words = tile("z2_words", [P, D], U32)
+        z2_scales = tile("z2_scales", [P, D], U8)
 
-        def query_quant(h):
-            quant(z2_w[:, half(h)], z2_s[:, half(h)], z2_bf[h][:].rearrange("p c t -> p (c t)"))
+        def query_product(s):
+            scaled_half(2 * s, w2_w, w2_s, xq_words[:, half(s)], xq_scales[:, half(s)], gq_sb,
+                        lambda t: z2_planes[s][:, t, :])
 
-        z_bf = [tile("z_bf%d" % j, [P, CH, PACK], BF16) for j in range(2)]
-        z_w = [tile("z_w%d" % j, [P, CH], U32) for j in range(2)]
-        z_s = [tile("z_s%d" % j, [P, CH], U8) for j in range(2)]
-        gk_b = gk_sb[:].unsqueeze(1).to_broadcast([P, CH, PACK])
+        def query_weave(s):
+            weave_planes(nc.vector.tensor_copy, z2_woven[s][:], z2_planes[s][:])
 
-        def key_product(j):
-            b = bank(4 + j)
-            for t in range(PACK):
-                mm(b[:, cols(t)], w1_w[:, cols(t)], w1_s[:, cols(t)], k_w[:, cols(j)], k_sc[:, cols(j)])
-            nc.vector.tensor_tensor(z_bf[j][:], b[:].rearrange("p (t c) -> p c t", t=PACK), gk_b, ALU.mult)
+        def query_quantise(s):
+            quantise(z2_words[:, half(s)], z2_scales[:, half(s)], z2_woven[s][:])
 
-        def key_quant(j):
-            quant(z_w[j][:], z_s[j][:], z_bf[j][:].rearrange("p c t -> p (c t)"))
+        z_woven = [tile("z_woven0", [P, CHUNK, SLOTS], BF16),
+                   tile("z_woven1", [P, CHUNK, SLOTS], BF16, after="z2_woven1")]
+        z_words = [tile("z_words%d" % j, [P, CHUNK], U32) for j in range(2)]
+        z_scales = [tile("z_scales%d" % j, [P, CHUNK], U8) for j in range(2)]
+        gk_over_columns = gk_sb[:].unsqueeze(1).unsqueeze(3).to_broadcast([P, CHUNK // 2, SLOTS, 2])
 
-        zl_pair = tile("zl_pair", [P, 2, H, 2], BF16)
-        zl_bf = tile("zl_bf", [P, H, 2], F32)
-        zl_w = tile("zl_w", [P, H], U32)
-        zl_s = tile("zl_s", [P, H], U8)
+        def early_key_product(j):
+            acc = bank(4 + j)
+            for t in range(SLOTS):
+                product(acc[:, chunk(t)], w1_w[:, chunk(t)], w1_s[:, chunk(t)],
+                        xk_words[:, chunk(j)], xk_scales[:, chunk(j)])
+            nc.vector.tensor_tensor(z_woven[j][:].rearrange("p (c n) t -> p c t n", n=2),
+                                    acc[:].rearrange("p (t c n) -> p c t n", t=SLOTS, n=2), gk_over_columns, ALU.mult)
 
-        def late_keys():
-            for u in range(2):
-                b = bank(6 + u)
-                for e in range(2):
-                    t = 2 * u + e
-                    mm(b[:, half(e)], w1_w[:, cols(t)], w1_s[:, cols(t)], k_w[:, half(1)], k_sc[:, half(1)])
-                for e in range(2):
-                    t = 2 * u + e
-                    nc.scalar.activation(zl_pair[:, u, :, e], b[:, half(e)], ACT.Copy, scale=gk_sb[:, t : t + 1])
+        def early_key_quantise(j):
+            quantise(z_words[j][:], z_scales[j][:], z_woven[j][:])
+
+        late_z_pairs = tile("late_z_pairs", [P, 2, HALF, 2], BF16)
+        late_z_woven = tile("late_z_woven", [P, HALF, SLOTS], BF16)
+        late_z_words = tile("late_z_words", [P, HALF], U32)
+        late_z_scales = tile("late_z_scales", [P, HALF], U8)
 
         query_product(0)
         query_product(1)
         query_weave(0)
-        key_product(0)
-        query_quant(0)
+        early_key_product(0)
+        query_quantise(0)
         query_weave(1)
-        key_quant(0)
-        query_quant(1)
-        key_product(1)
-        late_keys()
-        key_quant(1)
-        key_w = [z_w[0][:], z_w[1][:], zl_w[:, cols(0)], zl_w[:, cols(1)]]
-        key_s = [z_s[0][:], z_s[1][:], zl_s[:, cols(0)], zl_s[:, cols(1)]]
+        early_key_quantise(0)
+        query_quantise(1)
+        early_key_product(1)
+        scaled_half(6, w1_w, w1_s, xk_words[:, half(1)], xk_scales[:, half(1)], gk_sb,
+                    lambda t: late_z_pairs[:, t // 2, :, t % 2])
+        early_key_quantise(1)
+        key_words = [z_words[0][:], z_words[1][:], late_z_words[:, chunk(0)], late_z_words[:, chunk(1)]]
+        key_scales = [z_scales[0][:], z_scales[1][:], late_z_scales[:, chunk(0)], late_z_scales[:, chunk(1)]]
 
-        wv_bf = tile("wv_bf", [P, D, PACK], BF16)
-        wv_w = tile("wv_w", [P, D], U32)
-        wv_s = tile("wv_s", [P, D], U8)
+        wv_woven = tile("wv_woven", [P, D, SLOTS], BF16, after="z_words0")
+        wv_words = tile("wv_words", [P, D], U32)
+        wv_scales = tile("wv_scales", [P, D], U8)
+        shares = [tile("shares0", [P, D], F32), tile("shares1", [P, D], F32, after="wv_in"),
+                  tile("shares2", [P, D], F32, after="z_words0"), tile("shares3", [P, D], F32)]
+        fetched = [tile("fetched%d" % t, [P, PATCH], F32) for t in range(SLOTS)]
+        zp_pairs = tile("zp_pairs", [P, 2, D, 2], BF16, after="gi_sb")
+        zv_pairs = tile("zv_pairs", [P, 2, D, 2], BF16)
+        zv_woven = tile("zv_woven", [P, D, SLOTS], BF16)
+        zv_words = tile("zv_words", [P, D], U32)
+        zv_scales = tile("zv_scales", [P, D], U8)
 
-        p_sb = [tile("p%d" % j, [P, D], F32) for j in range(PACK)]
-        pg = [tile("pg%d" % j, [P, C], F32) for j in range(PACK)]
-        zp_pair = tile("zp_pair", [P, 2, D, 2], BF16)
-        zv_pair = tile("zv_pair", [P, 2, D, 2], BF16)
+        def score(t, bank_number, queries, width):
+            acc = bank(bank_number)
+            product(acc[:, 0:width], key_words[t], key_scales[t], z2_words[:, queries], z2_scales[:, queries])
+            nc.scalar.activation(shares[t][:, queries], acc[:, 0:width], ACT.Sigmoid, scale=SIXTEENTH)
 
-        def score(j):
-            b = bank(j)
-            mm(b[:], key_w[j], key_s[j], z2_w[:], z2_s[:])
-            nc.scalar.activation(p_sb[j][:], b[:], ACT.Sigmoid, scale=0.0625)
+        def fetch(t):
+            nc.vector.tensor_copy(fetched[t][:], shares[t][:].indirect(at_sb[:]))
 
-        def fetch(j):
-            nc.vector.tensor_copy(pg[j][:], p_sb[j][:].indirect(at_sb[:]))
+        def patch(t):
+            nc.vector.tensor_tensor(shares[t][:].indirect(at_sb[:]), fetched[t][:], fix_sb[t][:], ALU.mult)
 
-        def put(j):
-            nc.vector.tensor_tensor(p_sb[j][:].indirect(at_sb[:]), pg[j][:], fix_sb[:, j, :], ALU.mult)
-
-        def weigh(j):
-            nc.scalar.activation(zp_pair[:, j // 2, :, j % 2], p_sb[j][:], ACT.Copy, scale=gt_sb[:, j : j + 1])
+        def weigh(t, queries):
+            nc.scalar.activation(zp_pairs[:, t // 2, queries, t % 2], shares[t][:, queries], ACT.Copy,
+                                 scale=gt_sb[:, t, 0:1])
 
         def value(t):
-            b = bank(4 + t)
-            mm(b[:], k_w[:, cols(t)], k_sc[:, cols(t)], wv_w[:], wv_s[:])
-            nc.scalar.activation(
-                zv_pair[:, t // 2, :, t % 2].rearrange("p (u m) -> p u m", u=PACK),
-                b[:].rearrange("p (m u) -> p u m", u=PACK), ACT.Copy, scale=gi_sb[:, t : t + 1])
+            acc = bank(4 + t)
+            product(acc[:], xk_words[:, chunk(t)], xk_scales[:, chunk(t)], wv_words[:], wv_scales[:])
+            nc.scalar.activation(zv_pairs[:, t // 2, :, t % 2].rearrange("p (a c) -> p a c", a=SLOTS),
+                                 acc[:].rearrange("p (c a) -> p a c", a=SLOTS), ACT.Copy, scale=gi_sb[:, t, 0:1])
 
-        def wv_weave(h):
-            nc.scalar.copy(wv_bf[:, half(h), :], wv_raw[:, :, half(h)].rearrange("p j m -> p m j"))
-
-        score(0)
-        score(1)
-        nc.vector.tensor_copy(zl_bf[:], as_words(zl_pair).rearrange("p u c -> p c u"))
+        every = slice(0, D)
+        for s in range(2):
+            score(0, 2 * s, half(s), HALF)
+        weave_pairs(nc.vector.tensor_copy, late_z_woven[:], late_z_pairs[:])
         fetch(0)
-        quant(zl_w[:], zl_s[:], zl_bf[:].rearrange("p c u -> p (c u)").bitcast(BF16))
-        wv_weave(0)
-        wv_weave(1)
-        put(0)
+        quantise(late_z_words[:], late_z_scales[:], late_z_woven[:])
+        patch(0)
+        for s in range(2):
+            weave_planes(nc.scalar.copy, wv_woven[:, half(s), :], wv_in[:, :, half(s)])
+        quantise(wv_words[:], wv_scales[:], wv_woven[:])
+        score(1, 1, every, D)
         fetch(1)
-        score(2)
-        score(3)
-        quant(wv_w[:], wv_s[:], wv_bf[:].rearrange("p c t -> p (c t)"))
-        put(1)
+        patch(1)
+        score(2, 3, every, D)
+        score(3, 1, every, D)
+        for t in range(SLOTS):
+            value(t)
         fetch(2)
         fetch(3)
-        for t in range(PACK):
-            value(t)
-        put(2)
-        weigh(0)
-        weigh(1)
-        zv_bf = tile("zv_bf", [P, D, 2], F32)
-        nc.vector.tensor_copy(
-            zv_bf[:], zv_pair[:].rearrange("p u c e -> p u (c e)").bitcast(F32).rearrange("p u c -> p c u"))
-        weigh(2)
-        put(3)
-        zv_w = tile("zv_w", [P, D], U32)
-        zv_s = tile("zv_s", [P, D], U8)
-        quant(zv_w[:], zv_s[:], zv_bf[:].rearrange("p c u -> p (c u)").bitcast(BF16))
-        weigh(3)
+        patch(2)
+        weigh(0, every)
+        weigh(1, every)
+        weave_pairs(nc.vector.tensor_copy, zv_woven[:], zv_pairs[:])
+        weigh(2, every)
+        patch(3)
+        quantise(zv_words[:], zv_scales[:], zv_woven[:])
 
-        zp_words = zp_pair[:].rearrange("p u c e -> p u (c e)").bitcast(F32)
-        zp_bf = [tile("zp_bf%d" % h, [P, H, 2], F32) for h in range(2)]
-        zp_w = [tile("zp_w%d" % h, [P, H], U32) for h in range(2)]
-        zp_s = [tile("zp_s%d" % h, [P, H], U8) for h in range(2)]
-        for h in range(2):
-            nc.vector.tensor_copy(zp_bf[h][:], zp_words[:, :, h * H : (h + 1) * H].rearrange("p u c -> p c u"))
-        for h in range(2):
-            quant(zp_w[h][:], zp_s[h][:], zp_bf[h][:].rearrange("p c u -> p (c u)").bitcast(BF16))
+        zp_woven = [tile("zp_woven%d" % j, [P, CHUNK, SLOTS], BF16) for j in range(SLOTS)]
+        zp_words = [tile("zp_words%d" % j, [P, CHUNK], U32) for j in range(SLOTS)]
+        zp_scales = [tile("zp_scales%d" % j, [P, CHUNK], U8) for j in range(SLOTS)]
+        chunks = D // CHUNK
+        last_slot = SLOTS - 1
+        weigh(last_slot, chunk(0))
+        for j in range(chunks):
+            if j + 1 < chunks:
+                weigh(last_slot, chunk(j + 1))
+            weave_pairs(nc.scalar.copy, zp_woven[j][:], zp_pairs[:, :, chunk(j), :])
+            quantise(zp_words[j][:], zp_scales[j][:], zp_woven[j][:])
 
-        y_w = tile("y_w", [P, D], U32)
-        y_s = tile("y_s", [P, D], U8)
-        out_v = out_0.rearrange("(p t) v -> p t v", t=PACK)
-        y_bf = [tile("y_bf%d" % j, [P, CH, PACK], BF16) for j in range(PACK)]
+        y_words = tile("y_words", [P, D], U32)
+        y_scales = tile("y_scales", [P, D], U8)
+        y = tile("y", [P, SLOTS, D], F32)
+        y_woven = [tile("y_woven%d" % j, [P, CHUNK, SLOTS], BF16) for j in range(chunks)]
+        out_rows = out_0.rearrange("(p t) v -> p t v", t=SLOTS)
 
-        def out_chunk(j):
-            b = bank(j)
-            h, o = divmod(j, 2)
-            for t in range(PACK):
-                mm(b[:, cols(t)], zv_w[:, cols(t)], zv_s[:, cols(t)], zp_w[h][:, cols(o)], zp_s[h][:, cols(o)])
-            y = tile("y%d" % j, [P, PACK, CH], F32)
-            nc.vector.scalar_tensor_tensor(
-                y[:], b[:].rearrange("p (t c) -> p t c", t=PACK), 0.0625, res_sb[:, :, cols(j)], ALU.mult, ALU.add)
-            nc.sync.dma_start(out=out_v[:, :, cols(j)], in_=y[:])
-            nc.scalar.copy(y_bf[j][:], y[:].rearrange("p t c -> p c t"))
+        def out_product(j):
+            acc = bank(j)
+            for t in range(SLOTS):
+                product(acc[:, chunk(t)], zv_words[:, chunk(t)], zv_scales[:, chunk(t)], zp_words[j][:], zp_scales[j][:])
+            nc.vector.scalar_tensor_tensor(y[:, :, chunk(j)], acc[:].rearrange("p (t c) -> p t c", t=SLOTS), SIXTEENTH,
+                                           res_sb[:, :, chunk(j)], ALU.mult, ALU.add)
 
-        def out_quant(j):
-            quant(y_w[:, cols(j)], y_s[:, cols(j)], y_bf[j][:].rearrange("p c t -> p (c t)"))
+        def out_store(j):
+            nc.sync.dma_start(out=out_rows[:, :, chunk(j)], in_=y[:, :, chunk(j)])
 
-        out_chunk(0)
-        out_chunk(1)
-        out_chunk(2)
-        out_quant(0)
-        out_chunk(3)
-        out_quant(1)
-        out_quant(2)
-        out_quant(3)
-        nc.sync.dma_start(out=words_of(out_1), in_=y_w[:].bitcast(I32))
-        for q in range(4):
-            queue = nc.scalar if q % 2 else nc.sync
-            queue.dma_start(out=out_2[0, 4 * q : 4 * q + 4, :].bitcast(I32), in_=y_s[32 * q : 32 * q + 4, :].bitcast(I32))
+        def out_weave(j, copy):
+            weave_planes(copy, y_woven[j][:], y[:, :, chunk(j)])
+
+        def out_quantise(j):
+            quantise(y_words[:, chunk(j)], y_scales[:, chunk(j)], y_woven[j][:])
+
+        def store_words(queue, s):
+            queue.dma_start(out=words_of(out_1)[:, half(s)], in_=y_words[:, half(s)].bitcast(I32))
+
+        last_chunk = chunks - 1
+        for j in range(last_chunk):
+            out_product(j)
+            out_weave(j, nc.scalar.copy)
+            out_store(j)
+        out_product(last_chunk)
+        out_store(last_chunk)
+        out_quantise(0)
+        out_weave(last_chunk, nc.vector.tensor_copy)
+        out_quantise(1)
+        store_words(nc.scalar, 0)
+        out_quantise(2)
+        out_quantise(3)
+        store_words(nc.sync, 1)
+        for q in range(QUADRANTS):
+            queue = nc.sync if q % 2 else nc.scalar
+            queue.dma_start(out=out_2[0, 4 * q : 4 * q + 4, :].bitcast(I32),
+                            in_=y_scales[32 * q : 32 * q + 4, :].bitcast(I32))

from contextlib import ExitStack

import concourse.mybir as mybir

F32 = mybir.dt.float32
BF16 = mybir.dt.bfloat16
I32 = mybir.dt.int32
U32 = mybir.dt.uint32
U16 = mybir.dt.uint16
U8 = mybir.dt.uint8
FP8X4 = mybir.dt.float8_e4m3fn_x4
ACT = mybir.ActivationFunctionType
ALU = mybir.AluOpType

P = 128
SLOTS = 4
BLOCK_PARTS = 8
QUADRANTS = 4
LIST_ROWS = 16
TOKENS = 2048
D = 512
HALF = D // 2
CHUNK = 128
PATCH = 256
SIXTEENTH = 0.0625
FLOPS = 5 * 2 * D * D * D


def tile_picked_attpatch_sigmoid_po_kernel(
    tc, x_words, x_scales, w1_words, w1_scales, w2_words, w2_scales, gk, gq, fix, wv, gi, res, gt, offs, qs, at,
    out_0, out_1, out_2,
):
    nc = tc.nc
    with ExitStack() as ctx:
        sb = ctx.enter_context(tc.tile_pool(name="sb", bufs=1))
        ps = ctx.enter_context(tc.psum_pool(name="ps", bufs=1))

        def tile(name, shape, dtype, after=None):
            return sb.tile(shape, dtype, name=name, tag=after or name, align_bytes=64)

        def bank(number):
            return ps.tile([P, D], F32, name="bank%d" % number, tag="bank%d" % number)

        def chunk(j):
            return slice(j * CHUNK, (j + 1) * CHUNK)

        def half(s):
            return slice(s * HALF, (s + 1) * HALF)

        def words_of(dram):
            return dram[0].rearrange("p n t -> p (n t)").bitcast(I32)

        def product(out, lhs_words, lhs_scales, rhs_words, rhs_scales):
            nc.tensor.matmul_mx(out=out, lhsT=lhs_words.bitcast(FP8X4), lhsT_scale=lhs_scales,
                                rhs=rhs_words.bitcast(FP8X4), rhs_scale=rhs_scales, start=True, stop=True)

        def quantise(words, scales, woven):
            nc.vector.quantize_mx(out=words.bitcast(FP8X4), scales=scales, in_=woven.rearrange("p c t -> p (c t)"))

        def weave_planes(copy, woven, planes):
            copy(woven.rearrange("p (c n) t -> p c t n", n=4), planes.rearrange("p t (c n) -> p c t n", n=4))

        def weave_pairs(copy, woven, pairs):
            copy(woven.rearrange("p c t -> p (c t)").bitcast(F32).rearrange("p (c u) -> p c u", u=2),
                 pairs.rearrange("p u c e -> p u (c e)").bitcast(F32).rearrange("p u c -> p c u"))

        def load_scale_rows(queue, dst, dram):
            repeats = P // QUADRANTS // 4
            for q in range(QUADRANTS):
                rows = dram[0, 4 * q : 4 * q + 4, :].bitcast(I32)
                queue.dma_start(out=dst[32 * q : 32 * q + 32, :].bitcast(I32),
                                in_=rows.unsqueeze(0).broadcast_to([repeats, 4, dram.shape[2] // 4]))

        def load_feature_gain(name, dram):
            gain = tile(name, [P, SLOTS], F32)
            nc.gpsimd.dma_start(out=gain[:], in_=dram.rearrange("(p t) o -> p (t o)", t=SLOTS))
            return gain

        def load_entry_gain(name, dram):
            gain = tile(name, [P, SLOTS, 8], F32)
            rows = dram.rearrange("(b t r) o -> t b r o", t=SLOTS, r=BLOCK_PARTS)
            with nc.allow_non_contiguous_dma(reason="one value a partition"):
                for t in range(SLOTS):
                    nc.sync.dma_start(out=gain[:, t, 0:1], in_=rows[t])
            return gain

        offs_sb = tile("offs_sb", [P, D // LIST_ROWS], U16)
        qs_sb = tile("qs_sb", [P, D // LIST_ROWS], U16)
        at_sb = tile("at_sb", [P, PATCH // LIST_ROWS], U16)
        x_scale_table = tile("x_scale_table", [P, TOKENS], U8)
        w2_scales_in = tile("w2_scales_in", [P, D], U8)
        w1_scales_in = tile("w1_scales_in", [P, D], U8)

        warm = tile("warm", [P, 2], F32)
        nc.vector.memset(warm[:, 0:1], 0.0)
        nc.scalar.activation(warm[:, 1:2], warm[:, 0:1], ACT.Sigmoid)

        gq_sb = load_feature_gain("gq_sb", gq)
        gk_sb = load_feature_gain("gk_sb", gk)
        nc.sync.dma_start(qs_sb[:], qs)
        load_scale_rows(nc.sync, x_scale_table[:], x_scales)
        nc.sync.dma_start(offs_sb[:], offs)
        w2_words_in = tile("w2_words_in", [P, D], U32)
        nc.sync.dma_start(out=w2_words_in[:].bitcast(I32), in_=words_of(w2_words))
        x_word_table = tile("x_word_table", [P, TOKENS], U32)
        nc.sync.dma_start(out=x_word_table[:].bitcast(I32), in_=words_of(x_words))
        load_scale_rows(nc.scalar, w2_scales_in[:], w2_scales)
        w1_words_in = tile("w1_words_in", [P, D], U32)
        nc.sync.dma_start(out=w1_words_in[:].bitcast(I32), in_=words_of(w1_words))
        load_scale_rows(nc.sync, w1_scales_in[:], w1_scales)
        wv_in = tile("wv_in", [P, SLOTS, D], F32)
        nc.sync.dma_start(out=wv_in[:], in_=wv.rearrange("(p t) m -> p t m", t=SLOTS))
        nc.sync.dma_start(at_sb[:], at)
        fix_sb = [tile("fix%d" % t, [P, PATCH], F32) for t in range(SLOTS)]
        fix_rows = fix.rearrange("(b t r) c -> t b r c", t=SLOTS, r=BLOCK_PARTS)
        for t in range(SLOTS):
            nc.sync.dma_start(out=fix_sb[t][:], in_=fix_rows[t])
        res_sb = tile("res_sb", [P, SLOTS, D], F32)
        nc.sync.dma_start(out=res_sb[:], in_=res.rearrange("(p t) v -> p t v", t=SLOTS))
        gi_sb = load_entry_gain("gi_sb", gi)
        gt_sb = load_entry_gain("gt_sb", gt)

        def deal_weight_words(name, src, after=None):
            dealt = tile(name, [P, D], U32, after)
            nc.vector.tensor_copy(dealt[:].rearrange("p (t a n) -> p a t n", t=SLOTS, n=4),
                                  src.rearrange("p (a n t) -> p a t n", t=SLOTS, n=4))
            return dealt

        def deal_weight_scales(name, src):
            dealt = tile(name, [P, D], U8)
            nc.vector.tensor_copy(dealt[:].rearrange("p (t c) -> p t c", t=SLOTS),
                                  src.rearrange("p (c t) -> p t c", t=SLOTS))
            return dealt

        xq_scales = tile("xq_scales", [P, D], U8)
        nc.vector.tensor_copy(xq_scales[:], x_scale_table[:].indirect(qs_sb[:]))
        xk_scales_listed = tile("xk_scales_listed", [P, D], U8)
        nc.vector.tensor_copy(xk_scales_listed[:], x_scale_table[:].indirect(offs_sb[:]))
        w2_s = deal_weight_scales("w2_s", w2_scales_in[:])
        xk_scales = tile("xk_scales", [P, D], U8)
        nc.vector.tensor_copy(xk_scales[:].bitcast(I32).rearrange("p (t b w) -> p t b w", t=SLOTS, w=2),
                              xk_scales_listed[:].bitcast(I32).rearrange("p (b t w) -> p t b w", t=SLOTS, w=2))
        w2_w = deal_weight_words("w2_w", w2_words_in[:], after="w2_scales_in")
        xq_words = tile("xq_words", [P, D], U32, after="w2_words_in")
        list_half = HALF // LIST_ROWS
        for s in range(2):
            nc.vector.tensor_copy(xq_words[:, half(s)],
                                  x_word_table[:].indirect(qs_sb[:, s * list_half : (s + 1) * list_half]))
        xk_words = tile("xk_words", [P, D], U32)
        nc.vector.tensor_copy(xk_words[:].rearrange("p (t b r) -> p b t r", t=SLOTS, r=BLOCK_PARTS),
                              x_word_table[:].indirect(offs_sb[:]))
        w1_w = deal_weight_words("w1_w", w1_words_in[:])
        w1_s = deal_weight_scales("w1_s", w1_scales_in[:])

        def scaled_half(first_bank, weight_words, weight_scales, x_words_half, x_scales_half, gain, destination):
            for u in range(2):
                acc = bank(first_bank + u)
                for e in range(2):
                    t = 2 * u + e
                    product(acc[:, half(e)], weight_words[:, chunk(t)], weight_scales[:, chunk(t)],
                            x_words_half, x_scales_half)
                for e in range(2):
                    t = 2 * u + e
                    nc.scalar.activation(destination(t), acc[:, half(e)], ACT.Copy, scale=gain[:, t : t + 1])

        z2_planes = [tile("z2_planes%d" % s, [P, SLOTS, HALF], BF16) for s in range(2)]
        z2_woven = [tile("z2_woven0", [P, HALF, SLOTS], BF16, after="w1_scales_in"),
                    tile("z2_woven1", [P, HALF, SLOTS], BF16)]
        z2_words = tile("z2_words", [P, D], U32)
        z2_scales = tile("z2_scales", [P, D], U8)

        def query_product(s):
            scaled_half(2 * s, w2_w, w2_s, xq_words[:, half(s)], xq_scales[:, half(s)], gq_sb,
                        lambda t: z2_planes[s][:, t, :])

        def query_weave(s):
            weave_planes(nc.vector.tensor_copy, z2_woven[s][:], z2_planes[s][:])

        def query_quantise(s):
            quantise(z2_words[:, half(s)], z2_scales[:, half(s)], z2_woven[s][:])

        z_woven = [tile("z_woven0", [P, CHUNK, SLOTS], BF16),
                   tile("z_woven1", [P, CHUNK, SLOTS], BF16, after="z2_woven1")]
        z_words = [tile("z_words%d" % j, [P, CHUNK], U32) for j in range(2)]
        z_scales = [tile("z_scales%d" % j, [P, CHUNK], U8) for j in range(2)]
        gk_over_columns = gk_sb[:].unsqueeze(1).unsqueeze(3).to_broadcast([P, CHUNK // 2, SLOTS, 2])

        def early_key_product(j):
            acc = bank(4 + j)
            for t in range(SLOTS):
                product(acc[:, chunk(t)], w1_w[:, chunk(t)], w1_s[:, chunk(t)],
                        xk_words[:, chunk(j)], xk_scales[:, chunk(j)])
            nc.vector.tensor_tensor(z_woven[j][:].rearrange("p (c n) t -> p c t n", n=2),
                                    acc[:].rearrange("p (t c n) -> p c t n", t=SLOTS, n=2), gk_over_columns, ALU.mult)

        def early_key_quantise(j):
            quantise(z_words[j][:], z_scales[j][:], z_woven[j][:])

        late_z_pairs = tile("late_z_pairs", [P, 2, HALF, 2], BF16)
        late_z_woven = tile("late_z_woven", [P, HALF, SLOTS], BF16)
        late_z_words = tile("late_z_words", [P, HALF], U32)
        late_z_scales = tile("late_z_scales", [P, HALF], U8)

        query_product(0)
        query_product(1)
        query_weave(0)
        early_key_product(0)
        query_quantise(0)
        query_weave(1)
        early_key_quantise(0)
        query_quantise(1)
        early_key_product(1)
        scaled_half(6, w1_w, w1_s, xk_words[:, half(1)], xk_scales[:, half(1)], gk_sb,
                    lambda t: late_z_pairs[:, t // 2, :, t % 2])
        early_key_quantise(1)
        key_words = [z_words[0][:], z_words[1][:], late_z_words[:, chunk(0)], late_z_words[:, chunk(1)]]
        key_scales = [z_scales[0][:], z_scales[1][:], late_z_scales[:, chunk(0)], late_z_scales[:, chunk(1)]]

        wv_woven = tile("wv_woven", [P, D, SLOTS], BF16, after="z_words0")
        wv_words = tile("wv_words", [P, D], U32)
        wv_scales = tile("wv_scales", [P, D], U8)
        shares = [tile("shares0", [P, D], F32), tile("shares1", [P, D], F32, after="wv_in"),
                  tile("shares2", [P, D], F32, after="z_words0"), tile("shares3", [P, D], F32)]
        fetched = [tile("fetched%d" % t, [P, PATCH], F32) for t in range(SLOTS)]
        zp_pairs = tile("zp_pairs", [P, 2, D, 2], BF16, after="gi_sb")
        zv_pairs = tile("zv_pairs", [P, 2, D, 2], BF16)
        zv_woven = tile("zv_woven", [P, D, SLOTS], BF16)
        zv_words = tile("zv_words", [P, D], U32)
        zv_scales = tile("zv_scales", [P, D], U8)

        def score(t, bank_number, queries, width):
            acc = bank(bank_number)
            product(acc[:, 0:width], key_words[t], key_scales[t], z2_words[:, queries], z2_scales[:, queries])
            nc.scalar.activation(shares[t][:, queries], acc[:, 0:width], ACT.Sigmoid, scale=SIXTEENTH)

        def fetch(t):
            nc.vector.tensor_copy(fetched[t][:], shares[t][:].indirect(at_sb[:]))

        def patch(t):
            nc.vector.tensor_tensor(shares[t][:].indirect(at_sb[:]), fetched[t][:], fix_sb[t][:], ALU.mult)

        def weigh(t, queries):
            nc.scalar.activation(zp_pairs[:, t // 2, queries, t % 2], shares[t][:, queries], ACT.Copy,
                                 scale=gt_sb[:, t, 0:1])

        def value(t):
            acc = bank(4 + t)
            product(acc[:], xk_words[:, chunk(t)], xk_scales[:, chunk(t)], wv_words[:], wv_scales[:])
            nc.scalar.activation(zv_pairs[:, t // 2, :, t % 2].rearrange("p (a c) -> p a c", a=SLOTS),
                                 acc[:].rearrange("p (c a) -> p a c", a=SLOTS), ACT.Copy, scale=gi_sb[:, t, 0:1])

        every = slice(0, D)
        for s in range(2):
            score(0, 2 * s, half(s), HALF)
        weave_pairs(nc.vector.tensor_copy, late_z_woven[:], late_z_pairs[:])
        fetch(0)
        quantise(late_z_words[:], late_z_scales[:], late_z_woven[:])
        patch(0)
        for s in range(2):
            weave_planes(nc.scalar.copy, wv_woven[:, half(s), :], wv_in[:, :, half(s)])
        quantise(wv_words[:], wv_scales[:], wv_woven[:])
        score(1, 1, every, D)
        fetch(1)
        patch(1)
        score(2, 3, every, D)
        score(3, 1, every, D)
        for t in range(SLOTS):
            value(t)
        fetch(2)
        fetch(3)
        patch(2)
        weigh(0, every)
        weigh(1, every)
        weave_pairs(nc.vector.tensor_copy, zv_woven[:], zv_pairs[:])
        weigh(2, every)
        patch(3)
        quantise(zv_words[:], zv_scales[:], zv_woven[:])

        zp_woven = [tile("zp_woven%d" % j, [P, CHUNK, SLOTS], BF16) for j in range(SLOTS)]
        zp_words = [tile("zp_words%d" % j, [P, CHUNK], U32) for j in range(SLOTS)]
        zp_scales = [tile("zp_scales%d" % j, [P, CHUNK], U8) for j in range(SLOTS)]
        chunks = D // CHUNK
        last_slot = SLOTS - 1
        weigh(last_slot, chunk(0))
        for j in range(chunks):
            if j + 1 < chunks:
                weigh(last_slot, chunk(j + 1))
            weave_pairs(nc.scalar.copy, zp_woven[j][:], zp_pairs[:, :, chunk(j), :])
            quantise(zp_words[j][:], zp_scales[j][:], zp_woven[j][:])

        y_words = tile("y_words", [P, D], U32)
        y_scales = tile("y_scales", [P, D], U8)
        y = tile("y", [P, SLOTS, D], F32)
        y_woven = [tile("y_woven%d" % j, [P, CHUNK, SLOTS], BF16) for j in range(chunks)]
        out_rows = out_0.rearrange("(p t) v -> p t v", t=SLOTS)

        def out_product(j):
            acc = bank(j)
            for t in range(SLOTS):
                product(acc[:, chunk(t)], zv_words[:, chunk(t)], zv_scales[:, chunk(t)], zp_words[j][:], zp_scales[j][:])
            nc.vector.scalar_tensor_tensor(y[:, :, chunk(j)], acc[:].rearrange("p (t c) -> p t c", t=SLOTS), SIXTEENTH,
                                           res_sb[:, :, chunk(j)], ALU.mult, ALU.add)

        def out_store(j):
            nc.sync.dma_start(out=out_rows[:, :, chunk(j)], in_=y[:, :, chunk(j)])

        def out_weave(j, copy):
            weave_planes(copy, y_woven[j][:], y[:, :, chunk(j)])

        def out_quantise(j):
            quantise(y_words[:, chunk(j)], y_scales[:, chunk(j)], y_woven[j][:])

        def store_words(queue, s):
            queue.dma_start(out=words_of(out_1)[:, half(s)], in_=y_words[:, half(s)].bitcast(I32))

        last_chunk = chunks - 1
        for j in range(last_chunk):
            out_product(j)
            out_weave(j, nc.scalar.copy)
            out_store(j)
        out_product(last_chunk)
        out_store(last_chunk)
        out_quantise(0)
        out_weave(last_chunk, nc.vector.tensor_copy)
        out_quantise(1)
        store_words(nc.scalar, 0)
        out_quantise(2)
        out_quantise(3)
        store_words(nc.sync, 1)
        for q in range(QUADRANTS):
            queue = nc.sync if q % 2 else nc.scalar
            queue.dma_start(out=out_2[0, 4 * q : 4 * q + 4, :].bitcast(I32),
                            in_=y_scales[32 * q : 32 * q + 4, :].bitcast(I32))
